import numpy as np
import ml_dtypes


def mxq(x, axis, fmt="e4m3"):
    dtype, down = {"e4m3": (ml_dtypes.float8_e4m3fn, 7), "e5m2": (ml_dtypes.float8_e5m2, 14)}[fmt]
    v = np.moveaxis(np.asarray(x, np.float32).astype(ml_dtypes.bfloat16).astype(np.float64), axis, -1)
    blocks = v.reshape(v.shape[:-1] + (-1, 32))
    amax = np.abs(blocks).max(-1, keepdims=True)
    byte = np.maximum(np.where(amax > 0, np.frexp(amax)[1] - 1 + 127, 0) - down, 1)
    scale = np.exp2(byte - 127.0)
    codes = (blocks / scale).astype(np.float32).astype(dtype).astype(np.float64)
    return np.moveaxis((codes * scale).reshape(v.shape), -1, axis)


WIDE = False


def mx_kscale(k):
    if not WIDE:
        return np.ones(k)
    levels = np.array([10, -10, 5, -5, 0])
    if k % 512:
        return np.exp2(np.random.permutation(np.resize(levels, k // 32))).repeat(32)
    a = np.empty((k // 512, 16))
    for p in range(k // 512):
        a[p, :8] = np.random.permutation(np.resize(levels, 8))
        for g in range(8):
            far = levels[np.abs(levels - a[p, g]) >= 10]
            a[p, g + 8] = far[np.random.randint(len(far))]
    return np.exp2(a.ravel()).repeat(32)


def f64(x):
    return np.asarray(x).astype(np.float64)


def striped8(idx):
    return np.asarray(idx).reshape(8, -1, 16).transpose(0, 2, 1).reshape(128, -1).astype(np.uint16)


def unstriped8(offs):
    return offs.reshape(8, 16, -1).transpose(0, 2, 1).reshape(8, -1).astype(np.int64)


def pick8(x, idx, run):
    r = np.arange(len(x))
    return x[r[:, None], idx[r % (8 * run) // run]]


E2M1 = np.array([0.0, 0.5, 1.0, 1.5, 2.0, 3.0, 4.0, 6.0, -0.0, -0.5, -1.0, -1.5, -2.0, -3.0, -4.0, -6.0])


def pack_weight(w, fmt):
    k, n = w.shape
    w = f64(np.asarray(w, np.float32).astype(ml_dtypes.bfloat16)).reshape(k // 32, 32, n)
    amax = np.abs(w).max(1)
    if fmt == "e4m3":
        byte = np.frexp(amax)[1] - 1 + 127 - 7
    else:
        mant, ex = np.frexp(amax / 6.0)
        byte = np.where(mant > 0.5, ex, ex - 1) + 127
    byte = np.clip(np.where(amax > 0, byte, 1), 1, 254)
    scaled = (w * np.exp2(127.0 - byte)[:, None, :]).reshape(k, n).astype(np.float32)
    by_word = np.ascontiguousarray(scaled.reshape(k // 512, 128, 4, n).transpose(0, 1, 3, 2))
    if fmt == "e4m3":
        words = by_word.astype(ml_dtypes.float8_e4m3fn).view(np.uint8)
    else:
        c = by_word.astype(ml_dtypes.float4_e2m1fn).view(np.uint8) & 0xF
        words = (c[..., 0::2] | (c[..., 1::2] << 4)).reshape(k // 512, 128, 2 * n)
    return np.ascontiguousarray(words), np.ascontiguousarray(byte.astype(np.uint8).reshape(k // 512, 16, n))


def unpack_weight(words, scales, fmt):
    g, _, n = scales.shape
    words = np.ascontiguousarray(words).reshape(g, 128, n, -1)
    if fmt == "e4m3":
        vals = words.view(ml_dtypes.float8_e4m3fn).astype(np.float64)
    else:
        nib = np.empty((g, 128, n, 4), np.uint8)
        nib[..., 0::2] = words & 0xF
        nib[..., 1::2] = words >> 4
        vals = E2M1[nib]
    vals = vals * np.repeat(np.exp2(scales.astype(np.float64) - 127.0), 8, axis=1)[..., None]
    return vals.transpose(0, 1, 3, 2).reshape(g * 512, n)


D, T, U, I, Q = 512, 1024, 1024, 512, 128


def setup_inputs():
    n = np.random.standard_normal
    idx = np.stack([np.random.permutation(T)[:I] for _ in range(8)])
    idx2 = np.stack([np.random.permutation(T)[:I] for _ in range(8)])
    idx3 = np.stack([np.random.permutation(U)[:I] for _ in range(8)])
    idx4 = np.stack([np.random.permutation(U)[:I] for _ in range(8)])
    idx5 = np.stack([np.random.permutation(U)[:I] for _ in range(8)])
    fd = mx_kscale(D)
    cachep = pack_weight(n((D, T)) / fd[:, None], "e4m3")
    draftp = pack_weight(n((D, U)) / fd[:, None], "e2m1")
    return {
        "query": (n((D, Q)) * 1.0 / np.sqrt(D) * fd[:, None]).astype(np.float32),
        "cache_words": cachep[0],
        "cache_scales": cachep[1],
        "draft_words": draftp[0],
        "draft_scales": draftp[1],
        "offs": striped8(idx),
        "offs2": striped8(idx2),
        "offs3": striped8(idx3),
        "offs4": striped8(idx4),
        "offs5": striped8(idx5),
    }


def reference(query, cache_words, cache_scales, draft_words, draft_scales, offs, offs2, offs3, offs4, offs5):
    idx = unstriped8(offs)
    idx2 = unstriped8(offs2)
    idx3 = unstriped8(offs3)
    idx4 = unstriped8(offs4)
    idx5 = unstriped8(offs5)
    cacheu = unpack_weight(cache_words, cache_scales, "e4m3")
    draftu = unpack_weight(draft_words, draft_scales, "e2m1")
    queryq = mxq(f64(query), 0, "e4m3")
    a = queryq.T @ cacheu
    b = queryq.T @ draftu
    w = pick8(a, idx, 16) - pick8(a, idx2, 16)
    f1 = np.zeros((Q, U))
    f1[np.arange(Q)[:, None], idx3[np.arange(Q) % 128 // 16]] = w
    f2 = np.zeros((Q, U))
    f2[np.arange(Q)[:, None], idx4[np.arange(Q) % 128 // 16]] = pick8(a, idx, 16)
    m1 = np.maximum(f1, f2)
    bb = b - m1
    y = pick8(bb, idx5, 16)
    return y

@@ -1,0 +1,125 @@
+from contextlib import ExitStack
+
+import concourse.mybir as mybir
+
+D, T, U, I, Q = 512, 1024, 1024, 512, 128
+FLOPS = 2 * D * Q * (T + U)
+
+F32 = mybir.dt.float32
+BF16 = mybir.dt.bfloat16
+I32 = mybir.dt.int32
+U32 = mybir.dt.uint32
+U16 = mybir.dt.uint16
+U8 = mybir.dt.uint8
+FP8X4 = mybir.dt.float8_e4m3fn_x4
+FP4X4 = mybir.dt.float4_e2m1fn_x4
+COPY = mybir.ActivationFunctionType.Copy
+ALU = mybir.AluOpType
+
+P = 128
+PACK = 4
+HALF = I // 2
+LIST_COLS = I // 16
+
+
+def tile_attend_fetchedpair_two_kernel(tc, query, cache_words, cache_scales, draft_words, draft_scales,
+                                        offs, offs2, offs3, offs4, offs5, out):
+    nc = tc.nc
+    with ExitStack() as ctx:
+        sb = ctx.enter_context(tc.tile_pool(name="sb", bufs=1))
+        ps = ctx.enter_context(tc.psum_pool(name="ps", bufs=1))
+
+        def load_list(src, name):
+            t = sb.tile([P, LIST_COLS], U16, name=name)
+            nc.sync.dma_start(t[:], src)
+            return t
+
+        def load_scales(queue, plane, src):
+            for quad in range(4):
+                queue.dma_start(plane[32 * quad:32 * quad + 4, :].bitcast(I32),
+                                src[0, 4 * quad:4 * quad + 4, :].bitcast(I32))
+
+        cache_plane = sb.tile([P, T], U8, name="cache_plane", align_bytes=64)
+        draft_plane = sb.tile([P, U], U8, name="draft_plane", align_bytes=64)
+        f1 = sb.tile([P, U], F32, name="f1")
+        f2 = sb.tile([P, U], F32, name="f2")
+        nc.vector.memset(cache_plane[:].bitcast(I32), 0)
+
+        q_raw = sb.tile([P, PACK, Q], F32, name="q_raw")
+        nc.sync.dma_start(q_raw[:], query.rearrange("(p j) q -> p j q", j=PACK))
+        load_scales(nc.scalar, cache_plane, cache_scales)
+        cache_flat = cache_words[0].rearrange("p n t -> p (n t)")
+        cache_codes = []
+        for h in range(2):
+            t = sb.tile([P, T // 2], U32, name="cache_codes%d" % h, align_bytes=64)
+            nc.sync.dma_start(t[:].bitcast(I32), cache_flat[:, h * 2 * T:(h + 1) * 2 * T].bitcast(I32))
+            cache_codes.append(t)
+        idx = load_list(offs, "idx")
+        idx4 = load_list(offs4, "idx4")
+        idx2 = load_list(offs2, "idx2")
+        idx3 = load_list(offs3, "idx3")
+
+        nc.vector.memset(draft_plane[:].bitcast(I32), 0)
+        nc.vector.memset(f2[:], 0.0)
+        nc.vector.memset(f1[:], 0.0)
+
+        draft_codes = sb.tile([P, 2 * U], U8, name="draft_codes", align_bytes=64)
+        nc.sync.dma_start(draft_codes[:].bitcast(I32), draft_words[0].bitcast(I32))
+        load_scales(nc.sync, draft_plane, draft_scales)
+        idx5 = load_list(offs5, "idx5")
+
+        q_bf = sb.tile([P, Q, PACK], BF16, name="q_bf", align_bytes=64)
+        nc.vector.tensor_copy(q_bf[:].rearrange("p (c i) t -> p c t i", i=4),
+                              q_raw[:].rearrange("p t (c i) -> p c t i", i=4))
+        q_codes = sb.tile([P, Q], U32, name="q_codes", align_bytes=64)
+        q_plane = sb.tile([P, Q], U8, name="q_plane", align_bytes=64)
+        nc.vector.quantize_mx(out=q_codes[:].bitcast(FP8X4), scales=q_plane[:],
+                              in_=q_bf[:].rearrange("p q t -> p (q t)"))
+
+        a = sb.tile([P, T], F32, name="a")
+        N = 256
+        for c in range(T // N):
+            bank = ps.tile([P, N], F32, name="a_bank%d" % c)
+            h, c0 = divmod(c * N, T // 2)
+            nc.tensor.matmul_mx(out=bank[:], lhsT=q_codes[:].bitcast(FP8X4), lhsT_scale=q_plane[:],
+                                rhs=cache_codes[h][:, c0:c0 + N].bitcast(FP8X4),
+                                rhs_scale=cache_plane[:, c * N:(c + 1) * N], start=True, stop=True)
+            if c % 2 == 0:
+                nc.scalar.activation(a[:, c * N:(c + 1) * N], bank[:], COPY)
+            else:
+                nc.vector.tensor_copy(a[:, c * N:(c + 1) * N], bank[:])
+
+        b_banks = []
+        for c in range(2):
+            bank = ps.tile([P, 512], F32, name="b_bank%d" % c)
+            nc.tensor.matmul_mx(out=bank[:], lhsT=q_codes[:].bitcast(FP8X4), lhsT_scale=q_plane[:],
+                                rhs=draft_codes[:, c * 1024:(c + 1) * 1024].bitcast(FP4X4),
+                                rhs_scale=draft_plane[:, c * 512:(c + 1) * 512], start=True, stop=True)
+            b_banks.append(bank)
+
+        for h in range(2):
+            cols = slice(h * LIST_COLS // 2, (h + 1) * LIST_COLS // 2)
+            g1 = sb.tile([P, HALF], F32, name="g1_%d" % h)
+            g2 = sb.tile([P, HALF], F32, name="g2_%d" % h)
+            w = sb.tile([P, HALF], F32, name="w_%d" % h)
+            nc.vector.tensor_copy(g1[:], a[:].indirect(idx[:, cols]))
+            nc.scalar.activation(f2[:].indirect(idx4[:, cols]), g1[:], COPY)
+            nc.vector.tensor_copy(g2[:], a[:].indirect(idx2[:, cols]))
+            nc.vector.tensor_tensor(w[:], g1[:], g2[:], ALU.subtract)
+            nc.scalar.activation(f1[:].indirect(idx3[:, cols]), w[:], COPY)
+
+        m1 = sb.tile([P, U], F32, name="m1")
+        bb = sb.tile([P, U], F32, name="bb")
+        for c in range(2):
+            cs = slice(c * 512, (c + 1) * 512)
+            nc.vector.tensor_tensor(m1[:, cs], f1[:, cs], f2[:, cs], ALU.max)
+        for c in range(2):
+            cs = slice(c * 512, (c + 1) * 512)
+            nc.vector.tensor_tensor(bb[:, cs], b_banks[c][:], m1[:, cs], ALU.subtract)
+
+        y0 = sb.tile([P, HALF], F32, name="y0")
+        y1 = sb.tile([P, HALF], F32, name="y1")
+        nc.vector.tensor_copy(y0[:], bb[:].indirect(idx5[:, 0:LIST_COLS // 2]))
+        nc.scalar.activation(y1[:], bb[:].indirect(idx5[:, LIST_COLS // 2:LIST_COLS]), COPY)
+        nc.sync.dma_start(out[:, 0:HALF], y0[:])
+        nc.scalar.dma_start(out[:, HALF:I], y1[:])

@@ -69,25 +69,29 @@ def tile_attend_fetchedpair_two_kernel(tc, query, cache_words, cache_scales, dra
         idx5 = load_list(offs5, "idx5")
 
         q_bf = sb.tile([P, Q, PACK], BF16, name="q_bf", align_bytes=64)
-        nc.vector.tensor_copy(q_bf[:].rearrange("p (c i) t -> p c t i", i=4),
-                              q_raw[:].rearrange("p t (c i) -> p c t i", i=4))
         q_codes = sb.tile([P, Q], U32, name="q_codes", align_bytes=64)
         q_plane = sb.tile([P, Q], U8, name="q_plane", align_bytes=64)
-        nc.vector.quantize_mx(out=q_codes[:].bitcast(FP8X4), scales=q_plane[:],
-                              in_=q_bf[:].rearrange("p q t -> p (q t)"))
+        halves = [slice(0, Q // 2), slice(Q // 2, Q)]
+        for cols in halves:
+            nc.vector.tensor_copy(q_bf[:, cols, :].rearrange("p (c i) t -> p c t i", i=4),
+                                  q_raw[:, :, cols].rearrange("p t (c i) -> p c t i", i=4))
+        for cols in halves:
+            nc.vector.quantize_mx(out=q_codes[:, cols].bitcast(FP8X4), scales=q_plane[:, cols],
+                                  in_=q_bf[:, cols, :].rearrange("p q t -> p (q t)"))
 
         a = sb.tile([P, T], F32, name="a")
-        N = 256
-        for c in range(T // N):
-            bank = ps.tile([P, N], F32, name="a_bank%d" % c)
-            h, c0 = divmod(c * N, T // 2)
+        c0 = 0
+        for c, n in enumerate([256, 256, 256, 128, 128]):
+            bank = ps.tile([P, n], F32, name="a_bank%d" % c)
+            h, w0 = divmod(c0, T // 2)
             nc.tensor.matmul_mx(out=bank[:], lhsT=q_codes[:].bitcast(FP8X4), lhsT_scale=q_plane[:],
-                                rhs=cache_codes[h][:, c0:c0 + N].bitcast(FP8X4),
-                                rhs_scale=cache_plane[:, c * N:(c + 1) * N], start=True, stop=True)
+                                rhs=cache_codes[h][:, w0:w0 + n].bitcast(FP8X4),
+                                rhs_scale=cache_plane[:, c0:c0 + n], start=True, stop=True)
             if c % 2 == 0:
-                nc.scalar.activation(a[:, c * N:(c + 1) * N], bank[:], COPY)
+                nc.scalar.activation(a[:, c0:c0 + n], bank[:], COPY)
             else:
-                nc.vector.tensor_copy(a[:, c * N:(c + 1) * N], bank[:])
+                nc.vector.tensor_copy(a[:, c0:c0 + n], bank[:])
+            c0 = c0 + n
 
         b_banks = []
         for c in range(2):
@@ -97,16 +101,15 @@ def tile_attend_fetchedpair_two_kernel(tc, query, cache_words, cache_scales, dra
                                 rhs_scale=draft_plane[:, c * 512:(c + 1) * 512], start=True, stop=True)
             b_banks.append(bank)
 
-        for h in range(2):
-            cols = slice(h * LIST_COLS // 2, (h + 1) * LIST_COLS // 2)
-            g1 = sb.tile([P, HALF], F32, name="g1_%d" % h)
-            g2 = sb.tile([P, HALF], F32, name="g2_%d" % h)
-            w = sb.tile([P, HALF], F32, name="w_%d" % h)
-            nc.vector.tensor_copy(g1[:], a[:].indirect(idx[:, cols]))
-            nc.scalar.activation(f2[:].indirect(idx4[:, cols]), g1[:], COPY)
-            nc.vector.tensor_copy(g2[:], a[:].indirect(idx2[:, cols]))
-            nc.vector.tensor_tensor(w[:], g1[:], g2[:], ALU.subtract)
-            nc.scalar.activation(f1[:].indirect(idx3[:, cols]), w[:], COPY)
+        g1 = sb.tile([P, I], F32, name="g1")
+        g2 = sb.tile([P, I], F32, name="g2")
+        w = sb.tile([P, I], F32, name="w")
+        nc.vector.tensor_copy(g1[:, 0:HALF], a[:].indirect(idx[:, 0:LIST_COLS // 2]))
+        nc.scalar.activation(g1[:, HALF:I], a[:].indirect(idx[:, LIST_COLS // 2:LIST_COLS]), COPY)
+        nc.scalar.activation(f2[:].indirect(idx4[:]), g1[:], COPY)
+        nc.vector.tensor_copy(g2[:], a[:].indirect(idx2[:]))
+        nc.vector.tensor_tensor(w[:], g1[:], g2[:], ALU.subtract)
+        nc.scalar.activation(f1[:].indirect(idx3[:]), w[:], COPY)
 
         m1 = sb.tile([P, U], F32, name="m1")
         bb = sb.tile([P, U], F32, name="bb")

@@ -1,6 +1,7 @@
 from contextlib import ExitStack
 
 import concourse.mybir as mybir
+from concourse.masks import make_identity
 
 D, T, U, I, Q = 512, 1024, 1024, 512, 128
 FLOPS = 2 * D * Q * (T + U)
@@ -59,6 +60,9 @@ def tile_attend_fetchedpair_two_kernel(tc, query, cache_words, cache_scales, dra
         idx2 = load_list(offs2, "idx2")
         idx3 = load_list(offs3, "idx3")
 
+        ident = sb.tile([P, P], F32, name="ident")
+        nc.vector.memset(ident[:], 0.0)
+        make_identity(nc, ident[:], nomemset=True)
         nc.vector.memset(draft_plane[:].bitcast(I32), 0)
         nc.vector.memset(f2[:], 0.0)
         nc.vector.memset(f1[:], 0.0)
@@ -82,7 +86,7 @@ def tile_attend_fetchedpair_two_kernel(tc, query, cache_words, cache_scales, dra
         a = sb.tile([P, T], F32, name="a")
         c0 = 0
         for c, n in enumerate([256, 256, 256, 128, 128]):
-            bank = ps.tile([P, n], F32, name="a_bank%d" % c)
+            bank = ps.tile([P, n], F32, name="a_bank%d" % c, tag="bank%d" % c)
             h, w0 = divmod(c0, T // 2)
             nc.tensor.matmul_mx(out=bank[:], lhsT=q_codes[:].bitcast(FP8X4), lhsT_scale=q_plane[:],
                                 rhs=cache_codes[h][:, w0:w0 + n].bitcast(FP8X4),
@@ -93,13 +97,18 @@ def tile_attend_fetchedpair_two_kernel(tc, query, cache_words, cache_scales, dra
                 nc.vector.tensor_copy(a[:, c0:c0 + n], bank[:])
             c0 = c0 + n
 
-        b_banks = []
-        for c in range(2):
-            bank = ps.tile([P, 512], F32, name="b_bank%d" % c)
+        def draft_scores(bank, c0, n):
             nc.tensor.matmul_mx(out=bank[:], lhsT=q_codes[:].bitcast(FP8X4), lhsT_scale=q_plane[:],
-                                rhs=draft_codes[:, c * 1024:(c + 1) * 1024].bitcast(FP4X4),
-                                rhs_scale=draft_plane[:, c * 512:(c + 1) * 512], start=True, stop=True)
-            b_banks.append(bank)
+                                rhs=draft_codes[:, 2 * c0:2 * (c0 + n)].bitcast(FP4X4),
+                                rhs_scale=draft_plane[:, c0:c0 + n], start=True, stop=True)
+
+        b_lo = ps.tile([P, 512], F32, name="b_lo")
+        draft_scores(b_lo, 0, 512)
+        b_hi_ps = []
+        for c in range(2):
+            bank = ps.tile([P, 256], F32, name="b_hi_ps%d" % c, tag="turn%d" % c)
+            draft_scores(bank, 512 + 256 * c, 256)
+            b_hi_ps.append(bank)
 
         g1 = sb.tile([P, I], F32, name="g1")
         g2 = sb.tile([P, I], F32, name="g2")
@@ -111,14 +120,31 @@ def tile_attend_fetchedpair_two_kernel(tc, query, cache_words, cache_scales, dra
         nc.vector.tensor_tensor(w[:], g1[:], g2[:], ALU.subtract)
         nc.scalar.activation(f1[:].indirect(idx3[:]), w[:], COPY)
 
+        b_hi = sb.tile([P, 512], F32, name="b_hi")
+        for c in range(2):
+            nc.vector.tensor_copy(b_hi[:, 256 * c:256 * (c + 1)], b_hi_ps[c][:])
+
+        f2_ps = {}
+        for c in (1, 0):
+            turned_ps = ps.tile([P, 512], F32, name="turned_ps%d" % c, tag="turn%d" % (1 - c))
+            for j in range(4):
+                nc.tensor.transpose(turned_ps[:, j * P:(j + 1) * P], f2[:, c * 512 + j * P:c * 512 + (j + 1) * P], ident[:])
+            turned = sb.tile([P, 512], F32, name="turned%d" % c)
+            nc.vector.tensor_copy(turned[:], turned_ps[:])
+            back = ps.tile([P, 512], F32, name="f2_ps%d" % c, tag="bank%d" % c)
+            for j in range(4):
+                nc.tensor.transpose(back[:, j * P:(j + 1) * P], turned[:, j * P:(j + 1) * P], ident[:])
+            f2_ps[c] = back
+
         m1 = sb.tile([P, U], F32, name="m1")
         bb = sb.tile([P, U], F32, name="bb")
-        for c in range(2):
-            cs = slice(c * 512, (c + 1) * 512)
-            nc.vector.tensor_tensor(m1[:, cs], f1[:, cs], f2[:, cs], ALU.max)
-        for c in range(2):
-            cs = slice(c * 512, (c + 1) * 512)
-            nc.vector.tensor_tensor(bb[:, cs], b_banks[c][:], m1[:, cs], ALU.subtract)
+        for lo, hi in ((0, 192), (192, 512)):
+            nc.vector.tensor_tensor(m1[:, 512 + lo:512 + hi], f2_ps[1][:, lo:hi], f1[:, 512 + lo:512 + hi], ALU.max)
+            nc.gpsimd.tensor_tensor(bb[:, 512 + lo:512 + hi], b_hi[:, lo:hi], m1[:, 512 + lo:512 + hi], ALU.subtract)
+        for lo, hi in ((0, 256), (256, 512)):
+            nc.vector.tensor_tensor(m1[:, lo:hi], f2_ps[0][:, lo:hi], f1[:, lo:hi], ALU.max)
+        for lo, hi in ((0, 256), (256, 512)):
+            nc.vector.tensor_tensor(bb[:, lo:hi], b_lo[:, lo:hi], m1[:, lo:hi], ALU.subtract)
 
         y0 = sb.tile([P, HALF], F32, name="y0")
         y1 = sb.tile([P, HALF], F32, name="y1")

@@ -35,9 +35,9 @@ def tile_attend_fetchedpair_two_kernel(tc, query, cache_words, cache_scales, dra
             nc.sync.dma_start(t[:], src)
             return t
 
-        def load_scales(queue, plane, src):
+        def load_scales(queues, plane, src):
             for quad in range(4):
-                queue.dma_start(plane[32 * quad:32 * quad + 4, :].bitcast(I32),
+                queues[quad].dma_start(plane[32 * quad:32 * quad + 4, :].bitcast(I32),
                                 src[0, 4 * quad:4 * quad + 4, :].bitcast(I32))
 
         cache_plane = sb.tile([P, T], U8, name="cache_plane", align_bytes=64)
@@ -48,7 +48,7 @@ def tile_attend_fetchedpair_two_kernel(tc, query, cache_words, cache_scales, dra
 
         q_raw = sb.tile([P, PACK, Q], F32, name="q_raw")
         nc.sync.dma_start(q_raw[:], query.rearrange("(p j) q -> p j q", j=PACK))
-        load_scales(nc.scalar, cache_plane, cache_scales)
+        load_scales([nc.sync, nc.scalar, nc.sync, nc.scalar], cache_plane, cache_scales)
         cache_flat = cache_words[0].rearrange("p n t -> p (n t)")
         cache_codes = []
         for h in range(2):
@@ -69,7 +69,7 @@ def tile_attend_fetchedpair_two_kernel(tc, query, cache_words, cache_scales, dra
 
         draft_codes = sb.tile([P, 2 * U], U8, name="draft_codes", align_bytes=64)
         nc.sync.dma_start(draft_codes[:].bitcast(I32), draft_words[0].bitcast(I32))
-        load_scales(nc.sync, draft_plane, draft_scales)
+        load_scales([nc.sync] * 4, draft_plane, draft_scales)
         idx5 = load_list(offs5, "idx5")
 
         q_bf = sb.tile([P, Q, PACK], BF16, name="q_bf", align_bytes=64)
@@ -102,12 +102,15 @@ def tile_attend_fetchedpair_two_kernel(tc, query, cache_words, cache_scales, dra
                                 rhs=draft_codes[:, 2 * c0:2 * (c0 + n)].bitcast(FP4X4),
                                 rhs_scale=draft_plane[:, c0:c0 + n], start=True, stop=True)
 
-        b_lo = ps.tile([P, 512], F32, name="b_lo")
-        draft_scores(b_lo, 0, 512)
+        b_own = []
+        for c0, n, tag in ((0, 512, "b_lo"), (512, 128, "bank2")):
+            bank = ps.tile([P, n], F32, name="b_own%d" % c0, tag=tag)
+            draft_scores(bank, c0, n)
+            b_own.append(bank)
         b_hi_ps = []
-        for c in range(2):
-            bank = ps.tile([P, 256], F32, name="b_hi_ps%d" % c, tag="turn%d" % c)
-            draft_scores(bank, 512 + 256 * c, 256)
+        for c, (c0, n) in enumerate(((640, 256), (896, 128))):
+            bank = ps.tile([P, n], F32, name="b_hi_ps%d" % c, tag="turn%d" % c)
+            draft_scores(bank, c0, n)
             b_hi_ps.append(bank)
 
         g1 = sb.tile([P, I], F32, name="g1")
@@ -120,31 +123,38 @@ def tile_attend_fetchedpair_two_kernel(tc, query, cache_words, cache_scales, dra
         nc.vector.tensor_tensor(w[:], g1[:], g2[:], ALU.subtract)
         nc.scalar.activation(f1[:].indirect(idx3[:]), w[:], COPY)
 
-        b_hi = sb.tile([P, 512], F32, name="b_hi")
-        for c in range(2):
-            nc.vector.tensor_copy(b_hi[:, 256 * c:256 * (c + 1)], b_hi_ps[c][:])
+        b_hi = sb.tile([P, 384], F32, name="b_hi")
+        nc.vector.tensor_copy(b_hi[:, 0:256], b_hi_ps[0][:])
+        nc.vector.tensor_copy(b_hi[:, 256:384], b_hi_ps[1][:])
 
-        f2_ps = {}
-        for c in (1, 0):
-            turned_ps = ps.tile([P, 512], F32, name="turned_ps%d" % c, tag="turn%d" % (1 - c))
-            for j in range(4):
-                nc.tensor.transpose(turned_ps[:, j * P:(j + 1) * P], f2[:, c * 512 + j * P:c * 512 + (j + 1) * P], ident[:])
-            turned = sb.tile([P, 512], F32, name="turned%d" % c)
-            nc.vector.tensor_copy(turned[:], turned_ps[:])
-            back = ps.tile([P, 512], F32, name="f2_ps%d" % c, tag="bank%d" % c)
-            for j in range(4):
-                nc.tensor.transpose(back[:, j * P:(j + 1) * P], turned[:, j * P:(j + 1) * P], ident[:])
-            f2_ps[c] = back
+        own = ((0, 512), (512, 128))
+        turned = []
+        for c, blocks in enumerate(((0, 1, 2), (3, 4))):
+            bank = ps.tile([P, P * len(blocks)], F32, name="turned_ps%d" % c, tag="turn%d" % c)
+            for j, blk in enumerate(blocks):
+                nc.tensor.transpose(bank[:, j * P:(j + 1) * P], f2[:, blk * P:(blk + 1) * P], ident[:])
+            t = sb.tile([P, P * len(blocks)], F32, name="turned%d" % c, tag="turned%d" % c)
+            nc.vector.tensor_copy(t[:], bank[:])
+            turned.extend(t[:, j * P:(j + 1) * P] for j in range(len(blocks)))
+        f2_ps = []
+        for c, (c0, n) in enumerate(own):
+            bank = ps.tile([P, n], F32, name="f2_ps%d" % c, tag="bank%d" % c)
+            for j in range(0, n, P):
+                nc.tensor.transpose(bank[:, j:j + P], turned[(c0 + j) // P], ident[:])
+            f2_ps.append(bank)
 
-        m1 = sb.tile([P, U], F32, name="m1")
+        m1 = sb.tile([P, 640], F32, name="m1")
+        m1_hi = sb.tile([P, 384], F32, name="m1_hi", tag="turned0")
         bb = sb.tile([P, U], F32, name="bb")
-        for lo, hi in ((0, 192), (192, 512)):
-            nc.vector.tensor_tensor(m1[:, 512 + lo:512 + hi], f2_ps[1][:, lo:hi], f1[:, 512 + lo:512 + hi], ALU.max)
-            nc.gpsimd.tensor_tensor(bb[:, 512 + lo:512 + hi], b_hi[:, lo:hi], m1[:, 512 + lo:512 + hi], ALU.subtract)
-        for lo, hi in ((0, 256), (256, 512)):
-            nc.vector.tensor_tensor(m1[:, lo:hi], f2_ps[0][:, lo:hi], f1[:, lo:hi], ALU.max)
-        for lo, hi in ((0, 256), (256, 512)):
-            nc.vector.tensor_tensor(bb[:, lo:hi], b_lo[:, lo:hi], m1[:, lo:hi], ALU.subtract)
+        nc.vector.tensor_tensor(m1_hi[:], f2[:, 640:U], f1[:, 640:U], ALU.max)
+        nc.gpsimd.tensor_tensor(bb[:, 640:U], b_hi[:], m1_hi[:], ALU.subtract)
+        runs = ((0, 0, 256), (0, 256, 256), (1, 0, 128))
+        for c, lo, n in runs:
+            u0 = own[c][0] + lo
+            nc.vector.tensor_tensor(m1[:, u0:u0 + n], f2_ps[c][:, lo:lo + n], f1[:, u0:u0 + n], ALU.max)
+        for c, lo, n in runs:
+            u0 = own[c][0] + lo
+            nc.vector.tensor_tensor(bb[:, u0:u0 + n], b_own[c][:, lo:lo + n], m1[:, u0:u0 + n], ALU.subtract)
 
         y0 = sb.tile([P, HALF], F32, name="y0")
         y1 = sb.tile([P, HALF], F32, name="y1")

from contextlib import ExitStack

import concourse.mybir as mybir
from concourse.masks import make_identity

D, T, U, I, Q = 512, 1024, 1024, 512, 128
FLOPS = 2 * D * Q * (T + U)

F32 = mybir.dt.float32
BF16 = mybir.dt.bfloat16
I32 = mybir.dt.int32
U32 = mybir.dt.uint32
U16 = mybir.dt.uint16
U8 = mybir.dt.uint8
FP8X4 = mybir.dt.float8_e4m3fn_x4
FP4X4 = mybir.dt.float4_e2m1fn_x4
COPY = mybir.ActivationFunctionType.Copy
ALU = mybir.AluOpType

P = 128
PACK = 4
HALF = I // 2
LIST_COLS = I // 16


def tile_attend_fetchedpair_two_kernel(tc, query, cache_words, cache_scales, draft_words, draft_scales,
                                        offs, offs2, offs3, offs4, offs5, out):
    nc = tc.nc
    with ExitStack() as ctx:
        sb = ctx.enter_context(tc.tile_pool(name="sb", bufs=1))
        ps = ctx.enter_context(tc.psum_pool(name="ps", bufs=1))

        def load_list(src, name):
            t = sb.tile([P, LIST_COLS], U16, name=name)
            nc.sync.dma_start(t[:], src)
            return t

        def load_scales(queues, plane, src):
            for quad in range(4):
                queues[quad].dma_start(plane[32 * quad:32 * quad + 4, :].bitcast(I32),
                                src[0, 4 * quad:4 * quad + 4, :].bitcast(I32))

        cache_plane = sb.tile([P, T], U8, name="cache_plane", align_bytes=64)
        draft_plane = sb.tile([P, U], U8, name="draft_plane", align_bytes=64)
        f1 = sb.tile([P, U], F32, name="f1")
        f2 = sb.tile([P, U], F32, name="f2")
        nc.vector.memset(cache_plane[:].bitcast(I32), 0)

        q_raw = sb.tile([P, PACK, Q], F32, name="q_raw")
        nc.sync.dma_start(q_raw[:], query.rearrange("(p j) q -> p j q", j=PACK))
        load_scales([nc.sync, nc.scalar, nc.sync, nc.scalar], cache_plane, cache_scales)
        cache_flat = cache_words[0].rearrange("p n t -> p (n t)")
        cache_codes = []
        for h in range(2):
            t = sb.tile([P, T // 2], U32, name="cache_codes%d" % h, align_bytes=64)
            nc.sync.dma_start(t[:].bitcast(I32), cache_flat[:, h * 2 * T:(h + 1) * 2 * T].bitcast(I32))
            cache_codes.append(t)
        idx = load_list(offs, "idx")
        idx4 = load_list(offs4, "idx4")
        idx2 = load_list(offs2, "idx2")
        idx3 = load_list(offs3, "idx3")

        ident = sb.tile([P, P], F32, name="ident")
        nc.vector.memset(ident[:], 0.0)
        make_identity(nc, ident[:], nomemset=True)
        nc.vector.memset(draft_plane[:].bitcast(I32), 0)
        nc.vector.memset(f2[:], 0.0)
        nc.vector.memset(f1[:], 0.0)

        draft_codes = sb.tile([P, 2 * U], U8, name="draft_codes", align_bytes=64)
        nc.sync.dma_start(draft_codes[:].bitcast(I32), draft_words[0].bitcast(I32))
        load_scales([nc.sync] * 4, draft_plane, draft_scales)
        idx5 = load_list(offs5, "idx5")

        q_bf = sb.tile([P, Q, PACK], BF16, name="q_bf", align_bytes=64)
        q_codes = sb.tile([P, Q], U32, name="q_codes", align_bytes=64)
        q_plane = sb.tile([P, Q], U8, name="q_plane", align_bytes=64)
        halves = [slice(0, Q // 2), slice(Q // 2, Q)]
        for cols in halves:
            nc.vector.tensor_copy(q_bf[:, cols, :].rearrange("p (c i) t -> p c t i", i=4),
                                  q_raw[:, :, cols].rearrange("p t (c i) -> p c t i", i=4))
        for cols in halves:
            nc.vector.quantize_mx(out=q_codes[:, cols].bitcast(FP8X4), scales=q_plane[:, cols],
                                  in_=q_bf[:, cols, :].rearrange("p q t -> p (q t)"))

        a = sb.tile([P, T], F32, name="a")
        c0 = 0
        for c, n in enumerate([256, 256, 256, 128, 128]):
            bank = ps.tile([P, n], F32, name="a_bank%d" % c, tag="bank%d" % c)
            h, w0 = divmod(c0, T // 2)
            nc.tensor.matmul_mx(out=bank[:], lhsT=q_codes[:].bitcast(FP8X4), lhsT_scale=q_plane[:],
                                rhs=cache_codes[h][:, w0:w0 + n].bitcast(FP8X4),
                                rhs_scale=cache_plane[:, c0:c0 + n], start=True, stop=True)
            if c % 2 == 0:
                nc.scalar.activation(a[:, c0:c0 + n], bank[:], COPY)
            else:
                nc.vector.tensor_copy(a[:, c0:c0 + n], bank[:])
            c0 = c0 + n

        def draft_scores(bank, c0, n):
            nc.tensor.matmul_mx(out=bank[:], lhsT=q_codes[:].bitcast(FP8X4), lhsT_scale=q_plane[:],
                                rhs=draft_codes[:, 2 * c0:2 * (c0 + n)].bitcast(FP4X4),
                                rhs_scale=draft_plane[:, c0:c0 + n], start=True, stop=True)

        b_own = []
        for c0, n, tag in ((0, 512, "b_lo"), (512, 128, "bank2")):
            bank = ps.tile([P, n], F32, name="b_own%d" % c0, tag=tag)
            draft_scores(bank, c0, n)
            b_own.append(bank)
        b_hi_ps = []
        for c, (c0, n) in enumerate(((640, 256), (896, 128))):
            bank = ps.tile([P, n], F32, name="b_hi_ps%d" % c, tag="turn%d" % c)
            draft_scores(bank, c0, n)
            b_hi_ps.append(bank)

        g1 = sb.tile([P, I], F32, name="g1")
        g2 = sb.tile([P, I], F32, name="g2")
        w = sb.tile([P, I], F32, name="w")
        nc.vector.tensor_copy(g1[:, 0:HALF], a[:].indirect(idx[:, 0:LIST_COLS // 2]))
        nc.scalar.activation(g1[:, HALF:I], a[:].indirect(idx[:, LIST_COLS // 2:LIST_COLS]), COPY)
        nc.scalar.activation(f2[:].indirect(idx4[:]), g1[:], COPY)
        nc.vector.tensor_copy(g2[:], a[:].indirect(idx2[:]))
        nc.vector.tensor_tensor(w[:], g1[:], g2[:], ALU.subtract)
        nc.scalar.activation(f1[:].indirect(idx3[:]), w[:], COPY)

        b_hi = sb.tile([P, 384], F32, name="b_hi")
        nc.vector.tensor_copy(b_hi[:, 0:256], b_hi_ps[0][:])
        nc.vector.tensor_copy(b_hi[:, 256:384], b_hi_ps[1][:])

        own = ((0, 512), (512, 128))
        turned = []
        for c, blocks in enumerate(((0, 1, 2), (3, 4))):
            bank = ps.tile([P, P * len(blocks)], F32, name="turned_ps%d" % c, tag="turn%d" % c)
            for j, blk in enumerate(blocks):
                nc.tensor.transpose(bank[:, j * P:(j + 1) * P], f2[:, blk * P:(blk + 1) * P], ident[:])
            t = sb.tile([P, P * len(blocks)], F32, name="turned%d" % c, tag="turned%d" % c)
            nc.vector.tensor_copy(t[:], bank[:])
            turned.extend(t[:, j * P:(j + 1) * P] for j in range(len(blocks)))
        f2_ps = []
        for c, (c0, n) in enumerate(own):
            bank = ps.tile([P, n], F32, name="f2_ps%d" % c, tag="bank%d" % c)
            for j in range(0, n, P):
                nc.tensor.transpose(bank[:, j:j + P], turned[(c0 + j) // P], ident[:])
            f2_ps.append(bank)

        m1 = sb.tile([P, 640], F32, name="m1")
        m1_hi = sb.tile([P, 384], F32, name="m1_hi", tag="turned0")
        bb = sb.tile([P, U], F32, name="bb")
        nc.vector.tensor_tensor(m1_hi[:], f2[:, 640:U], f1[:, 640:U], ALU.max)
        nc.gpsimd.tensor_tensor(bb[:, 640:U], b_hi[:], m1_hi[:], ALU.subtract)
        runs = ((0, 0, 256), (0, 256, 256), (1, 0, 128))
        for c, lo, n in runs:
            u0 = own[c][0] + lo
            nc.vector.tensor_tensor(m1[:, u0:u0 + n], f2_ps[c][:, lo:lo + n], f1[:, u0:u0 + n], ALU.max)
        for c, lo, n in runs:
            u0 = own[c][0] + lo
            nc.vector.tensor_tensor(bb[:, u0:u0 + n], b_own[c][:, lo:lo + n], m1[:, u0:u0 + n], ALU.subtract)

        y0 = sb.tile([P, HALF], F32, name="y0")
        y1 = sb.tile([P, HALF], F32, name="y1")
        nc.vector.tensor_copy(y0[:], bb[:].indirect(idx5[:, 0:LIST_COLS // 2]))
        nc.scalar.activation(y1[:], bb[:].indirect(idx5[:, LIST_COLS // 2:LIST_COLS]), COPY)
        nc.sync.dma_start(out[:, 0:HALF], y0[:])
        nc.scalar.dma_start(out[:, HALF:I], y1[:])
